import numpy as np
import ml_dtypes


def mxq(x, axis, fmt="e4m3"):
    dtype, down = {"e4m3": (ml_dtypes.float8_e4m3fn, 7), "e5m2": (ml_dtypes.float8_e5m2, 14)}[fmt]
    v = np.moveaxis(np.asarray(x, np.float32).astype(ml_dtypes.bfloat16).astype(np.float64), axis, -1)
    blocks = v.reshape(v.shape[:-1] + (-1, 32))
    amax = np.abs(blocks).max(-1, keepdims=True)
    byte = np.maximum(np.where(amax > 0, np.frexp(amax)[1] - 1 + 127, 0) - down, 1)
    scale = np.exp2(byte - 127.0)
    codes = (blocks / scale).astype(np.float32).astype(dtype).astype(np.float64)
    return np.moveaxis((codes * scale).reshape(v.shape), -1, axis)


WIDE = False


def mx_kscale(k):
    if not WIDE:
        return np.ones(k)
    levels = np.array([10, -10, 5, -5, 0])
    if k % 512:
        return np.exp2(np.random.permutation(np.resize(levels, k // 32))).repeat(32)
    a = np.empty((k // 512, 16))
    for p in range(k // 512):
        a[p, :8] = np.random.permutation(np.resize(levels, 8))
        for g in range(8):
            far = levels[np.abs(levels - a[p, g]) >= 10]
            a[p, g + 8] = far[np.random.randint(len(far))]
    return np.exp2(a.ravel()).repeat(32)


def f64(x):
    return np.asarray(x).astype(np.float64)


def striped(idx):
    return np.tile(np.asarray(idx).reshape(-1, 16).T, (8, 1)).astype(np.uint16)


def unstriped(offs):
    return offs[:16].T.reshape(-1).astype(np.int64)


def striped8(idx):
    return np.asarray(idx).reshape(8, -1, 16).transpose(0, 2, 1).reshape(128, -1).astype(np.uint16)


def unstriped8(offs):
    return offs.reshape(8, 16, -1).transpose(0, 2, 1).reshape(8, -1).astype(np.int64)


def pick8(x, idx, run):
    r = np.arange(len(x))
    return x[r[:, None], idx[r % (8 * run) // run]]


E2M1 = np.array([0.0, 0.5, 1.0, 1.5, 2.0, 3.0, 4.0, 6.0, -0.0, -0.5, -1.0, -1.5, -2.0, -3.0, -4.0, -6.0])


def pack_weight(w, fmt):
    k, n = w.shape
    w = f64(np.asarray(w, np.float32).astype(ml_dtypes.bfloat16)).reshape(k // 32, 32, n)
    amax = np.abs(w).max(1)
    if fmt == "e4m3":
        byte = np.frexp(amax)[1] - 1 + 127 - 7
    else:
        mant, ex = np.frexp(amax / 6.0)
        byte = np.where(mant > 0.5, ex, ex - 1) + 127
    byte = np.clip(np.where(amax > 0, byte, 1), 1, 254)
    scaled = (w * np.exp2(127.0 - byte)[:, None, :]).reshape(k, n).astype(np.float32)
    by_word = np.ascontiguousarray(scaled.reshape(k // 512, 128, 4, n).transpose(0, 1, 3, 2))
    if fmt == "e4m3":
        words = by_word.astype(ml_dtypes.float8_e4m3fn).view(np.uint8)
    else:
        c = by_word.astype(ml_dtypes.float4_e2m1fn).view(np.uint8) & 0xF
        words = (c[..., 0::2] | (c[..., 1::2] << 4)).reshape(k // 512, 128, 2 * n)
    return np.ascontiguousarray(words), np.ascontiguousarray(byte.astype(np.uint8).reshape(k // 512, 16, n))


def unpack_weight(words, scales, fmt):
    g, _, n = scales.shape
    words = np.ascontiguousarray(words).reshape(g, 128, n, -1)
    if fmt == "e4m3":
        vals = words.view(ml_dtypes.float8_e4m3fn).astype(np.float64)
    else:
        nib = np.empty((g, 128, n, 4), np.uint8)
        nib[..., 0::2] = words & 0xF
        nib[..., 1::2] = words >> 4
        vals = E2M1[nib]
    vals = vals * np.repeat(np.exp2(scales.astype(np.float64) - 127.0), 8, axis=1)[..., None]
    return vals.transpose(0, 1, 3, 2).reshape(g * 512, n)


K, J, R, T, F, G, O, C, S, N = 512, 512, 512, 1024, 1024, 1024, 256, 512, 256, 256


def setup_inputs():
    n = np.random.standard_normal
    idx = np.random.permutation(T)[:J]
    idx2 = np.stack([np.random.permutation(F)[:R] for _ in range(8)])
    idx3 = np.stack([np.random.permutation(G)[:R] for _ in range(8)])
    idx4 = np.stack([np.random.permutation(J)[:S] for _ in range(8)])
    idx5 = np.stack([np.random.permutation(C)[:S] for _ in range(8)])
    idx6 = np.stack([np.random.permutation(C)[:O] for _ in range(8)])
    idx7 = np.random.permutation(T)[:O]
    fk = mx_kscale(K)
    fr = mx_kscale(R)
    xtp = pack_weight(n((K, T)) * fk[:, None], "e2m1")
    wbp = pack_weight(n((R, N)) * 1 / np.sqrt(R) / fr[:, None], "e2m1")
    wsp = pack_weight(n((K, N)) * 1 / np.sqrt(K) / fk[:, None], "e4m3")
    return {
        "xt_words": xtp[0],
        "xt_scales": xtp[1],
        "ua": (np.random.randint(-7, 8, (K, F)).astype(np.float64)).astype(np.float32),
        "ub": (np.random.randint(-7, 8, (K, G)).astype(np.float64)).astype(np.float32),
        "ha": ((np.random.randint(10, 25, (K, 1)) / 1024.0) / fk[:, None]).astype(np.float32),
        "hb": ((np.random.randint(4, 13, (K, 1)) / 1024.0) / fk[:, None]).astype(np.float32),
        "sa": (np.random.uniform(0.5, 1.6, (R, 1)) * fr[:, None]).astype(np.float32),
        "sb": (np.random.uniform(0.5, 1.6, (R, 1))).astype(np.float32),
        "wb_words": wbp[0],
        "wb_scales": wbp[1],
        "ws_words": wsp[0],
        "ws_scales": wsp[1],
        "offs": striped(idx),
        "offs2": striped8(idx2),
        "offs3": striped8(idx3),
        "offs4": striped8(idx4),
        "offs5": striped8(idx5),
        "offs6": striped8(idx6),
        "offs7": striped(idx7),
    }


def reference(xt_words, xt_scales, ua, ub, ha, hb, sa, sb, wb_words, wb_scales, ws_words, ws_scales, offs, offs2, offs3, offs4, offs5, offs6, offs7):
    idx = unstriped(offs)
    idx2 = unstriped8(offs2)
    idx3 = unstriped8(offs3)
    idx4 = unstriped8(offs4)
    idx5 = unstriped8(offs5)
    idx6 = unstriped8(offs6)
    idx7 = unstriped(offs7)
    xtu = unpack_weight(xt_words, xt_scales, "e2m1")
    wbu = unpack_weight(wb_words, wb_scales, "e2m1")
    wsu = unpack_weight(ws_words, ws_scales, "e4m3")
    wc = pick8(f64(ua), idx2, 64) * f64(ha) + pick8(f64(ub), idx3, 64) * f64(hb)
    wcq = mxq(wc, 0, "e4m3")
    xtidxg = xtu[:, idx]
    a = wcq.T @ xtidxg
    h1 = pick8(a, idx4, 64) * f64(sa)
    pw = np.zeros((R, C))
    pw[np.arange(R)[:, None], idx5[np.arange(R) % 512 // 64]] = h1
    g1 = np.maximum(pw, 0.0)
    hid = pick8(g1, idx6, 64) * f64(sb)
    hidq = mxq(hid, 0, "e4m3")
    xtidx7g = xtu[:, idx7]
    y = wbu.T @ hidq + wsu.T @ xtidx7g
    return y

@@ -1,0 +1,197 @@
+from contextlib import ExitStack
+
+import concourse.mybir as mybir
+
+K, J, R, T, F, O, C, S, N = 512, 512, 512, 1024, 1024, 256, 512, 256, 256
+FLOPS = 2 * K * R * J + 2 * R * N * O + 2 * K * N * O
+
+F32 = mybir.dt.float32
+BF16 = mybir.dt.bfloat16
+I32 = mybir.dt.int32
+U32 = mybir.dt.uint32
+U16 = mybir.dt.uint16
+U8 = mybir.dt.uint8
+FP8X4 = mybir.dt.float8_e4m3fn_x4
+FP4X4 = mybir.dt.float4_e2m1fn_x4
+COPY = mybir.ActivationFunctionType.Copy
+RELU = mybir.ActivationFunctionType.Relu
+ADD = mybir.AluOpType.add
+
+P = 128
+PACK = 4
+
+
+def tile_picked_tokens_twobooks_one_weighedposting_further_plain_kernel(
+    tc, xt_words, xt_scales, ua, ub, ha, hb, sa, sb, wb_words, wb_scales, ws_words, ws_scales,
+    offs, offs2, offs3, offs4, offs5, offs6, offs7, out,
+):
+    nc = tc.nc
+    with ExitStack() as ctx:
+        keep = ctx.enter_context(tc.tile_pool(name="keep", bufs=1))
+        psum = ctx.enter_context(tc.psum_pool(name="psum", bufs=1))
+
+        def load_list(src, name):
+            tile = keep.tile(list(src.shape), U16, name=name)
+            nc.sync.dma_start(tile[:], src)
+            return tile
+
+        def load_factors(queue, src, name):
+            tile = keep.tile([P, PACK], F32, name=name)
+            queue.dma_start(tile[:], src.rearrange("(p t) one -> p (t one)", t=PACK))
+            return tile
+
+        def load_table(src, j, name):
+            tile = keep.tile([P, F], F32, name=name)
+            nc.sync.dma_start(tile[:], src.rearrange("(p t) f -> p t f", t=PACK)[:, j, :])
+            return tile
+
+        xs_win = keep.tile([P, T], U8, name="xs_win", align_bytes=64)
+        nc.vector.memset(xs_win[:].bitcast(I32), 0)
+        ws_sc = keep.tile([P, N], U8, name="ws_sc", align_bytes=64)
+        wb_sc = keep.tile([P, N], U8, name="wb_sc", align_bytes=64)
+        nc.vector.memset(ws_sc[:].bitcast(I32), 0)
+        nc.vector.memset(wb_sc[:].bitcast(I32), 0)
+        boards = [keep.tile([P, C], F32, name=f"board{t}") for t in range(PACK)]
+        for t in range(PACK):
+            nc.vector.memset(boards[t][:], 0.0)
+
+        ha_t = load_factors(nc.scalar, ha, "ha_t")
+        hb_t = load_factors(nc.scalar, hb, "hb_t")
+        xs_stage = keep.tile([4, 4, T // 4], I32, name="xs_stage")
+        nc.scalar.dma_start(xs_stage[:], xt_scales[0].bitcast(I32).rearrange("(q i) c -> i q c", i=4))
+        ua_t, ub_t = [], []
+        ua_t.append(load_table(ua, 0, "ua0"))
+        l2 = load_list(offs2, "l2")
+        ub_t.append(load_table(ub, 0, "ub0"))
+        l3 = load_list(offs3, "l3")
+        ua_t.append(load_table(ua, 1, "ua1"))
+        l1 = load_list(offs, "l1")
+        l7 = load_list(offs7, "l7")
+        xw_win = keep.tile([P, T], U16, name="xw_win", align_bytes=64)
+        nc.sync.dma_start(xw_win[:].bitcast(I32), xt_words[0].bitcast(I32))
+        ub_t.append(load_table(ub, 1, "ub1"))
+        for j in (2, 3):
+            ua_t.append(load_table(ua, j, f"ua{j}"))
+            ub_t.append(load_table(ub, j, f"ub{j}"))
+        sa_t = load_factors(nc.sync, sa, "sa_t")
+        l4 = load_list(offs4, "l4")
+        l5 = load_list(offs5, "l5")
+        l6 = load_list(offs6, "l6")
+        sb_t = load_factors(nc.sync, sb, "sb_t")
+        ws_w = keep.tile([P, N], U32, name="ws_w", align_bytes=64)
+        nc.sync.dma_start(ws_w[:].bitcast(I32), ws_words[0].rearrange("p n t -> p (n t)").bitcast(I32))
+        for q in range(4):
+            nc.sync.dma_start(ws_sc[32 * q : 32 * q + 4, :].bitcast(I32), ws_scales[0][4 * q : 4 * q + 4, :].bitcast(I32))
+        wb_w = keep.tile([P, 2 * N], U8, name="wb_w", align_bytes=64)
+        nc.sync.dma_start(wb_w[:].bitcast(I32), wb_words[0].bitcast(I32))
+        for q in range(4):
+            nc.sync.dma_start(wb_sc[32 * q : 32 * q + 4, :].bitcast(I32), wb_scales[0][4 * q : 4 * q + 4, :].bitcast(I32))
+
+        for q in range(4):
+            nc.vector.tensor_copy(xs_win[32 * q : 32 * q + 4, :].bitcast(I32), xs_stage[:, q, :])
+        slot_w = keep.tile([P, J], U16, name="slot_w", align_bytes=64)
+        slot_s = keep.tile([P, J], U8, name="slot_s", align_bytes=64)
+        place_w = keep.tile([P, O], U16, name="place_w", align_bytes=64)
+        place_s = keep.tile([P, O], U8, name="place_s", align_bytes=64)
+        nc.vector.tensor_copy(slot_s[:], xs_win[:].indirect(l1[:]))
+        nc.vector.tensor_copy(place_s[:], xs_win[:].indirect(l7[:]))
+        nc.vector.tensor_copy(slot_w[:], xw_win[:].indirect(l1[:]))
+        nc.vector.tensor_copy(place_w[:], xw_win[:].indirect(l7[:]))
+
+        ga = [keep.tile([P, 2, R], F32, name=f"ga{u}") for u in range(2)]
+        gb = [keep.tile([P, 2, R], F32, name=f"gb{u}") for u in range(2)]
+        wc = keep.tile([P, R, PACK], BF16, name="wc", align_bytes=64)
+        wc_v = wc[:].rearrange("p (t m) j -> p m t j", t=PACK)
+        H = R // 2
+        for j in range(PACK):
+            u, e = divmod(j, 2)
+            nc.scalar.activation(ga[u][:, e, :], ua_t[j][:].indirect(l2[:]), COPY, scale=ha_t[:, j : j + 1])
+            if j < PACK - 1:
+                nc.scalar.activation(gb[u][:, e, :], ub_t[j][:].indirect(l3[:]), COPY, scale=hb_t[:, j : j + 1])
+            else:
+                for h in range(2):
+                    nc.scalar.activation(gb[u][:, e, h * H : (h + 1) * H], ub_t[j][:].indirect(l3[:, h * 16 : (h + 1) * 16]), COPY, scale=hb_t[:, j : j + 1])
+            if j == 1:
+                nc.vector.tensor_tensor(
+                    wc_v[:, :, :, 0:2],
+                    ga[0][:].rearrange("p e (m t) -> p m t e", t=PACK),
+                    gb[0][:].rearrange("p e (m t) -> p m t e", t=PACK), ADD)
+        ga_v = ga[1][:].rearrange("p e (m t) -> p m t e", t=PACK)
+        gb_v = gb[1][:].rearrange("p e (m t) -> p m t e", t=PACK)
+
+        wc_w = [keep.tile([P, P], U32, name=f"wc_w{t}", align_bytes=64) for t in range(PACK)]
+        wc_s = [keep.tile([P, P], U8, name=f"wc_s{t}", align_bytes=64) for t in range(PACK)]
+        for t in range(PACK):
+            if t % 2 == 0:
+                for h in range(2):
+                    ms, ts = slice(64 * h, 64 * h + 64), slice(t, t + 2)
+                    nc.vector.tensor_tensor(
+                        wc_v[:, ms, ts, 2:4].rearrange("p m t e -> p m e t"),
+                        ga_v[:, ms, ts, :].rearrange("p m t e -> p m e t"),
+                        gb_v[:, ms, ts, :].rearrange("p m t e -> p m e t"), ADD)
+            nc.vector.quantize_mx(
+                out=wc_w[t][:].bitcast(FP8X4), scales=wc_s[t][:],
+                in_=wc[:, t * P : (t + 1) * P, :].rearrange("p m j -> p (m j)"))
+
+        kepts = []
+        for t in range(PACK):
+            a_sb = keep.tile([P, J], F32, name=f"a_sb{t}", tag="rows", bufs=2, align_bytes=64)
+            pieces = 2 if t == 0 else 1
+            w = J // pieces
+            for i in range(pieces):
+                bank = psum.tile([P, w], F32, name=f"a_ps{t}_{i}")
+                nc.tensor.matmul_mx(
+                    out=bank[:], lhsT=wc_w[t][:].bitcast(FP8X4), lhsT_scale=wc_s[t][:],
+                    rhs=slot_w[:, i * w : (i + 1) * w].bitcast(FP4X4), rhs_scale=slot_s[:, i * w : (i + 1) * w],
+                    start=True, stop=True)
+                if t == 1:
+                    nc.vector.tensor_copy(a_sb[:, i * w : (i + 1) * w], bank[:])
+                else:
+                    nc.scalar.copy(a_sb[:, i * w : (i + 1) * w], bank[:])
+            h1 = keep.tile([P, S], F32, name=f"h1_{t}")
+            nc.scalar.activation(h1[:], a_sb[:].indirect(l4[:]), COPY, scale=sa_t[:, t : t + 1])
+            if t == 0:
+                nc.vector.tensor_copy(boards[t][:].indirect(l5[:]), h1[:])
+            else:
+                kept = keep.tile([P, S], F32, name=f"kept{t}")
+                kepts.append(kept)
+                nc.scalar.activation(kept[:], h1[:], RELU)
+                nc.vector.tensor_copy(boards[t][:].indirect(l5[:]), kept[:])
+        g1_0 = keep.tile([P, C], F32, name="g1_0", tag="rows", bufs=2, align_bytes=64)
+        nc.scalar.activation(g1_0[:], boards[0][:], RELU)
+        g1 = [g1_0] + boards[1:]
+
+        banks = [psum.tile([P, 2, P], F32, name=f"y_ps{h}") for h in range(2)]
+        for h in range(2):
+            for b in range(2):
+                nc.tensor.matmul_mx(
+                    out=banks[h][:, b, :], lhsT=ws_w[:, b * P : (b + 1) * P].bitcast(FP8X4), lhsT_scale=ws_sc[:, b * P : (b + 1) * P],
+                    rhs=place_w[:, h * P : (h + 1) * P].bitcast(FP4X4), rhs_scale=place_s[:, h * P : (h + 1) * P],
+                    start=(b == 0), stop=False)
+
+        hid = keep.tile([P, PACK, O], BF16, name="hid", tag="rows", bufs=2, align_bytes=64)
+        for t in range(PACK - 1):
+            nc.scalar.activation(hid[:, t, :], g1[t][:].indirect(l6[:]), COPY, scale=sb_t[:, t : t + 1])
+        t = PACK - 1
+        for h in range(2):
+            nc.scalar.activation(hid[:, t, h * P : (h + 1) * P], g1[t][:].indirect(l6[:, 8 * h : 8 * h + 8]), COPY, scale=sb_t[:, t : t + 1])
+        woven = [keep.tile([P, P, PACK], BF16, name=f"woven{h}", align_bytes=64) for h in range(2)]
+        hid_w = [keep.tile([P, P], U32, name=f"hid_w{h}", align_bytes=64) for h in range(2)]
+        hid_s = [keep.tile([P, P], U8, name=f"hid_s{h}", align_bytes=64) for h in range(2)]
+        out_v = out.rearrange("(b p) o -> p b o", p=P)
+        for h in range(2):
+            nc.vector.tensor_copy(
+                woven[h][:].rearrange("p (c i) t -> p c t i", i=4),
+                hid[:, :, h * P : (h + 1) * P].rearrange("p t (c i) -> p c t i", i=4))
+            nc.vector.quantize_mx(out=hid_w[h][:].bitcast(FP8X4), scales=hid_s[h][:], in_=woven[h][:].rearrange("p o t -> p (o t)"))
+            for b in range(2):
+                nc.tensor.matmul_mx(
+                    out=banks[h][:, b, :], lhsT=wb_w[:, 2 * b * P : 2 * (b + 1) * P].bitcast(FP4X4), lhsT_scale=wb_sc[:, b * P : (b + 1) * P],
+                    rhs=hid_w[h][:].bitcast(FP8X4), rhs_scale=hid_s[h][:],
+                    start=False, stop=(b == 1))
+            y_sb = keep.tile([P, 2, P], F32, name=f"y_sb{h}")
+            if h == 0:
+                nc.scalar.copy(y_sb[:], banks[h][:])
+            else:
+                nc.vector.tensor_copy(y_sb[:], banks[h][:])
+            nc.sync.dma_start(out_v[:, :, h * P : (h + 1) * P], y_sb[:])

@@ -19,6 +19,12 @@ ADD = mybir.AluOpType.add
 
 P = 128
 PACK = 4
+QUADS = 4
+QUAD = 32
+SCALE_ROWS = 4
+LIST_COL = 16
+ALIGN = 64
+LAST = PACK - 1
 
 
 def tile_picked_tokens_twobooks_one_weighedposting_further_plain_kernel(
@@ -37,161 +43,180 @@ def tile_picked_tokens_twobooks_one_weighedposting_further_plain_kernel(
 
         def load_factors(queue, src, name):
             tile = keep.tile([P, PACK], F32, name=name)
-            queue.dma_start(tile[:], src.rearrange("(p t) one -> p (t one)", t=PACK))
+            queue.dma_start(tile[:], src.rearrange("(p j) one -> p (j one)", j=PACK))
             return tile
 
-        def load_table(src, j, name):
+        def load_plane(src, j, name):
             tile = keep.tile([P, F], F32, name=name)
-            nc.sync.dma_start(tile[:], src.rearrange("(p t) f -> p t f", t=PACK)[:, j, :])
+            nc.sync.dma_start(tile[:], src.rearrange("(p j) f -> p j f", j=PACK)[:, j, :])
             return tile
 
-        xs_win = keep.tile([P, T], U8, name="xs_win", align_bytes=64)
-        nc.vector.memset(xs_win[:].bitcast(I32), 0)
-        ws_sc = keep.tile([P, N], U8, name="ws_sc", align_bytes=64)
-        wb_sc = keep.tile([P, N], U8, name="wb_sc", align_bytes=64)
-        nc.vector.memset(ws_sc[:].bitcast(I32), 0)
-        nc.vector.memset(wb_sc[:].bitcast(I32), 0)
+        def load_scale_rows(tile, src):
+            for q in range(QUADS):
+                nc.sync.dma_start(
+                    tile[QUAD * q : QUAD * q + SCALE_ROWS, :].bitcast(I32),
+                    src[0][SCALE_ROWS * q : SCALE_ROWS * (q + 1), :].bitcast(I32))
+
+        def fetch_scaled(dst, window, offsets, factors, plane):
+            nc.scalar.activation(dst, window[:].indirect(offsets), COPY, scale=factors[:, plane : plane + 1])
+
+        def list_half(tile, entries, half):
+            cols = entries // 2 // LIST_COL
+            return tile[:, half * cols : (half + 1) * cols]
+
+        warm_in = keep.tile([P, 1], F32, name="warm_in")
+        warm_out = keep.tile([P, 1], F32, name="warm_out")
+        nc.vector.memset(warm_in[:], 0.0)
+        nc.scalar.activation(warm_out[:], warm_in[:], COPY)
+
+        xt_s = keep.tile([P, T], U8, name="xt_s", align_bytes=ALIGN)
+        nc.vector.memset(xt_s[:].bitcast(I32), 0)
+        ws_s = keep.tile([P, N], U8, name="ws_s", align_bytes=ALIGN)
+        wb_s = keep.tile([P, N], U8, name="wb_s", align_bytes=ALIGN)
+        nc.vector.memset(ws_s[:].bitcast(I32), 0)
+        nc.vector.memset(wb_s[:].bitcast(I32), 0)
         boards = [keep.tile([P, C], F32, name=f"board{t}") for t in range(PACK)]
         for t in range(PACK):
             nc.vector.memset(boards[t][:], 0.0)
 
         ha_t = load_factors(nc.scalar, ha, "ha_t")
         hb_t = load_factors(nc.scalar, hb, "hb_t")
-        xs_stage = keep.tile([4, 4, T // 4], I32, name="xs_stage")
-        nc.scalar.dma_start(xs_stage[:], xt_scales[0].bitcast(I32).rearrange("(q i) c -> i q c", i=4))
+        xt_s_stage = keep.tile([SCALE_ROWS, QUADS, T // 4], I32, name="xt_s_stage")
+        nc.scalar.dma_start(xt_s_stage[:], xt_scales[0].bitcast(I32).rearrange("(q i) c -> i q c", i=SCALE_ROWS))
         ua_t, ub_t = [], []
-        ua_t.append(load_table(ua, 0, "ua0"))
-        l2 = load_list(offs2, "l2")
-        ub_t.append(load_table(ub, 0, "ub0"))
-        l3 = load_list(offs3, "l3")
-        ua_t.append(load_table(ua, 1, "ua1"))
-        l1 = load_list(offs, "l1")
-        l7 = load_list(offs7, "l7")
-        xw_win = keep.tile([P, T], U16, name="xw_win", align_bytes=64)
-        nc.sync.dma_start(xw_win[:].bitcast(I32), xt_words[0].bitcast(I32))
-        ub_t.append(load_table(ub, 1, "ub1"))
-        for j in (2, 3):
-            ua_t.append(load_table(ua, j, f"ua{j}"))
-            ub_t.append(load_table(ub, j, f"ub{j}"))
+        ua_t.append(load_plane(ua, 0, "ua0"))
+        idx2 = load_list(offs2, "idx2")
+        ub_t.append(load_plane(ub, 0, "ub0"))
+        idx3 = load_list(offs3, "idx3")
+        ua_t.append(load_plane(ua, 1, "ua1"))
+        idx = load_list(offs, "idx")
+        idx7 = load_list(offs7, "idx7")
+        xt_w = keep.tile([P, T], U16, name="xt_w", align_bytes=ALIGN)
+        nc.sync.dma_start(xt_w[:].bitcast(I32), xt_words[0].bitcast(I32))
+        ub_t.append(load_plane(ub, 1, "ub1"))
+        for j in range(2, PACK):
+            ua_t.append(load_plane(ua, j, f"ua{j}"))
+            ub_t.append(load_plane(ub, j, f"ub{j}"))
         sa_t = load_factors(nc.sync, sa, "sa_t")
-        l4 = load_list(offs4, "l4")
-        l5 = load_list(offs5, "l5")
-        l6 = load_list(offs6, "l6")
+        idx4 = load_list(offs4, "idx4")
+        idx5 = load_list(offs5, "idx5")
+        idx6 = load_list(offs6, "idx6")
         sb_t = load_factors(nc.sync, sb, "sb_t")
-        ws_w = keep.tile([P, N], U32, name="ws_w", align_bytes=64)
+        ws_w = keep.tile([P, N], U32, name="ws_w", align_bytes=ALIGN)
         nc.sync.dma_start(ws_w[:].bitcast(I32), ws_words[0].rearrange("p n t -> p (n t)").bitcast(I32))
-        for q in range(4):
-            nc.sync.dma_start(ws_sc[32 * q : 32 * q + 4, :].bitcast(I32), ws_scales[0][4 * q : 4 * q + 4, :].bitcast(I32))
-        wb_w = keep.tile([P, 2 * N], U8, name="wb_w", align_bytes=64)
+        load_scale_rows(ws_s, ws_scales)
+        wb_w = keep.tile([P, 2 * N], U8, name="wb_w", align_bytes=ALIGN)
         nc.sync.dma_start(wb_w[:].bitcast(I32), wb_words[0].bitcast(I32))
-        for q in range(4):
-            nc.sync.dma_start(wb_sc[32 * q : 32 * q + 4, :].bitcast(I32), wb_scales[0][4 * q : 4 * q + 4, :].bitcast(I32))
+        load_scale_rows(wb_s, wb_scales)
 
-        for q in range(4):
-            nc.vector.tensor_copy(xs_win[32 * q : 32 * q + 4, :].bitcast(I32), xs_stage[:, q, :])
-        slot_w = keep.tile([P, J], U16, name="slot_w", align_bytes=64)
-        slot_s = keep.tile([P, J], U8, name="slot_s", align_bytes=64)
-        place_w = keep.tile([P, O], U16, name="place_w", align_bytes=64)
-        place_s = keep.tile([P, O], U8, name="place_s", align_bytes=64)
-        nc.vector.tensor_copy(slot_s[:], xs_win[:].indirect(l1[:]))
-        nc.vector.tensor_copy(place_s[:], xs_win[:].indirect(l7[:]))
-        nc.vector.tensor_copy(slot_w[:], xw_win[:].indirect(l1[:]))
-        nc.vector.tensor_copy(place_w[:], xw_win[:].indirect(l7[:]))
+        for q in range(QUADS):
+            nc.vector.tensor_copy(xt_s[QUAD * q : QUAD * q + SCALE_ROWS, :].bitcast(I32), xt_s_stage[:, q, :])
+        slot_w = keep.tile([P, J], U16, name="slot_w", align_bytes=ALIGN)
+        slot_s = keep.tile([P, J], U8, name="slot_s", align_bytes=ALIGN)
+        place_w = keep.tile([P, O], U16, name="place_w", align_bytes=ALIGN)
+        place_s = keep.tile([P, O], U8, name="place_s", align_bytes=ALIGN)
+        nc.vector.tensor_copy(slot_s[:], xt_s[:].indirect(idx[:]))
+        nc.vector.tensor_copy(place_s[:], xt_s[:].indirect(idx7[:]))
+        nc.vector.tensor_copy(slot_w[:], xt_w[:].indirect(idx[:]))
+        nc.vector.tensor_copy(place_w[:], xt_w[:].indirect(idx7[:]))
 
-        ga = [keep.tile([P, 2, R], F32, name=f"ga{u}") for u in range(2)]
-        gb = [keep.tile([P, 2, R], F32, name=f"gb{u}") for u in range(2)]
-        wc = keep.tile([P, R, PACK], BF16, name="wc", align_bytes=64)
+        from_a = [keep.tile([P, 2, R], F32, name=f"from_a{u}") for u in range(2)]
+        from_b = [keep.tile([P, 2, R], F32, name=f"from_b{u}") for u in range(2)]
+        wc = keep.tile([P, R, PACK], BF16, name="wc", align_bytes=ALIGN)
         wc_v = wc[:].rearrange("p (t m) j -> p m t j", t=PACK)
-        H = R // 2
+        a_v = [tile[:].rearrange("p e (m t) -> p m t e", t=PACK) for tile in from_a]
+        b_v = [tile[:].rearrange("p e (m t) -> p m t e", t=PACK) for tile in from_b]
+        half_r = R // 2
         for j in range(PACK):
             u, e = divmod(j, 2)
-            nc.scalar.activation(ga[u][:, e, :], ua_t[j][:].indirect(l2[:]), COPY, scale=ha_t[:, j : j + 1])
-            if j < PACK - 1:
-                nc.scalar.activation(gb[u][:, e, :], ub_t[j][:].indirect(l3[:]), COPY, scale=hb_t[:, j : j + 1])
+            fetch_scaled(from_a[u][:, e, :], ua_t[j], idx2[:], ha_t, j)
+            if j < LAST:
+                fetch_scaled(from_b[u][:, e, :], ub_t[j], idx3[:], hb_t, j)
             else:
-                for h in range(2):
-                    nc.scalar.activation(gb[u][:, e, h * H : (h + 1) * H], ub_t[j][:].indirect(l3[:, h * 16 : (h + 1) * 16]), COPY, scale=hb_t[:, j : j + 1])
+                for half in range(2):
+                    fetch_scaled(from_b[u][:, e, half * half_r : (half + 1) * half_r], ub_t[j],
+                                 list_half(idx3, R, half), hb_t, j)
             if j == 1:
-                nc.vector.tensor_tensor(
-                    wc_v[:, :, :, 0:2],
-                    ga[0][:].rearrange("p e (m t) -> p m t e", t=PACK),
-                    gb[0][:].rearrange("p e (m t) -> p m t e", t=PACK), ADD)
-        ga_v = ga[1][:].rearrange("p e (m t) -> p m t e", t=PACK)
-        gb_v = gb[1][:].rearrange("p e (m t) -> p m t e", t=PACK)
+                nc.vector.tensor_tensor(wc_v[:, :, :, 0:2], a_v[0], b_v[0], ADD)
 
-        wc_w = [keep.tile([P, P], U32, name=f"wc_w{t}", align_bytes=64) for t in range(PACK)]
-        wc_s = [keep.tile([P, P], U8, name=f"wc_s{t}", align_bytes=64) for t in range(PACK)]
+        wc_w = [keep.tile([P, P], U32, name=f"wc_w{t}", align_bytes=ALIGN) for t in range(PACK)]
+        wc_s = [keep.tile([P, P], U8, name=f"wc_s{t}", align_bytes=ALIGN) for t in range(PACK)]
+        half_m = P // 2
         for t in range(PACK):
             if t % 2 == 0:
-                for h in range(2):
-                    ms, ts = slice(64 * h, 64 * h + 64), slice(t, t + 2)
+                for half in range(2):
+                    ms, ts = slice(half * half_m, (half + 1) * half_m), slice(t, t + 2)
                     nc.vector.tensor_tensor(
                         wc_v[:, ms, ts, 2:4].rearrange("p m t e -> p m e t"),
-                        ga_v[:, ms, ts, :].rearrange("p m t e -> p m e t"),
-                        gb_v[:, ms, ts, :].rearrange("p m t e -> p m e t"), ADD)
+                        a_v[1][:, ms, ts, :].rearrange("p m t e -> p m e t"),
+                        b_v[1][:, ms, ts, :].rearrange("p m t e -> p m e t"), ADD)
             nc.vector.quantize_mx(
                 out=wc_w[t][:].bitcast(FP8X4), scales=wc_s[t][:],
                 in_=wc[:, t * P : (t + 1) * P, :].rearrange("p m j -> p (m j)"))
 
-        kepts = []
         for t in range(PACK):
-            a_sb = keep.tile([P, J], F32, name=f"a_sb{t}", tag="rows", bufs=2, align_bytes=64)
+            a_sb = keep.tile([P, J], F32, name=f"a_sb{t}", tag="rows", bufs=2, align_bytes=ALIGN)
             pieces = 2 if t == 0 else 1
-            w = J // pieces
+            width = J // pieces
             for i in range(pieces):
-                bank = psum.tile([P, w], F32, name=f"a_ps{t}_{i}")
+                cols = slice(i * width, (i + 1) * width)
+                a_ps = psum.tile([P, width], F32, name=f"a_ps{t}_{i}")
                 nc.tensor.matmul_mx(
-                    out=bank[:], lhsT=wc_w[t][:].bitcast(FP8X4), lhsT_scale=wc_s[t][:],
-                    rhs=slot_w[:, i * w : (i + 1) * w].bitcast(FP4X4), rhs_scale=slot_s[:, i * w : (i + 1) * w],
+                    out=a_ps[:], lhsT=wc_w[t][:].bitcast(FP8X4), lhsT_scale=wc_s[t][:],
+                    rhs=slot_w[:, cols].bitcast(FP4X4), rhs_scale=slot_s[:, cols],
                     start=True, stop=True)
                 if t == 1:
-                    nc.vector.tensor_copy(a_sb[:, i * w : (i + 1) * w], bank[:])
+                    nc.vector.tensor_copy(a_sb[:, cols], a_ps[:])
                 else:
-                    nc.scalar.copy(a_sb[:, i * w : (i + 1) * w], bank[:])
+                    nc.scalar.copy(a_sb[:, cols], a_ps[:])
             h1 = keep.tile([P, S], F32, name=f"h1_{t}")
-            nc.scalar.activation(h1[:], a_sb[:].indirect(l4[:]), COPY, scale=sa_t[:, t : t + 1])
+            fetch_scaled(h1[:], a_sb, idx4[:], sa_t, t)
             if t == 0:
-                nc.vector.tensor_copy(boards[t][:].indirect(l5[:]), h1[:])
+                nc.vector.tensor_copy(boards[t][:].indirect(idx5[:]), h1[:])
             else:
-                kept = keep.tile([P, S], F32, name=f"kept{t}")
-                kepts.append(kept)
-                nc.scalar.activation(kept[:], h1[:], RELU)
-                nc.vector.tensor_copy(boards[t][:].indirect(l5[:]), kept[:])
-        g1_0 = keep.tile([P, C], F32, name="g1_0", tag="rows", bufs=2, align_bytes=64)
+                h1_pos = keep.tile([P, S], F32, name=f"h1_pos{t}")
+                nc.scalar.activation(h1_pos[:], h1[:], RELU)
+                nc.vector.tensor_copy(boards[t][:].indirect(idx5[:]), h1_pos[:])
+        g1_0 = keep.tile([P, C], F32, name="g1_0", tag="rows", bufs=2, align_bytes=ALIGN)
         nc.scalar.activation(g1_0[:], boards[0][:], RELU)
         g1 = [g1_0] + boards[1:]
 
-        banks = [psum.tile([P, 2, P], F32, name=f"y_ps{h}") for h in range(2)]
-        for h in range(2):
+        y_ps = [psum.tile([P, 2, P], F32, name=f"y_ps{half}") for half in range(2)]
+        for half in range(2):
+            places = slice(half * P, (half + 1) * P)
             for b in range(2):
                 nc.tensor.matmul_mx(
-                    out=banks[h][:, b, :], lhsT=ws_w[:, b * P : (b + 1) * P].bitcast(FP8X4), lhsT_scale=ws_sc[:, b * P : (b + 1) * P],
-                    rhs=place_w[:, h * P : (h + 1) * P].bitcast(FP4X4), rhs_scale=place_s[:, h * P : (h + 1) * P],
+                    out=y_ps[half][:, b, :],
+                    lhsT=ws_w[:, b * P : (b + 1) * P].bitcast(FP8X4), lhsT_scale=ws_s[:, b * P : (b + 1) * P],
+                    rhs=place_w[:, places].bitcast(FP4X4), rhs_scale=place_s[:, places],
                     start=(b == 0), stop=False)
 
-        hid = keep.tile([P, PACK, O], BF16, name="hid", tag="rows", bufs=2, align_bytes=64)
-        for t in range(PACK - 1):
-            nc.scalar.activation(hid[:, t, :], g1[t][:].indirect(l6[:]), COPY, scale=sb_t[:, t : t + 1])
-        t = PACK - 1
-        for h in range(2):
-            nc.scalar.activation(hid[:, t, h * P : (h + 1) * P], g1[t][:].indirect(l6[:, 8 * h : 8 * h + 8]), COPY, scale=sb_t[:, t : t + 1])
-        woven = [keep.tile([P, P, PACK], BF16, name=f"woven{h}", align_bytes=64) for h in range(2)]
-        hid_w = [keep.tile([P, P], U32, name=f"hid_w{h}", align_bytes=64) for h in range(2)]
-        hid_s = [keep.tile([P, P], U8, name=f"hid_s{h}", align_bytes=64) for h in range(2)]
+        hid = keep.tile([P, PACK, O], BF16, name="hid", tag="rows", bufs=2, align_bytes=ALIGN)
+        for t in range(LAST):
+            fetch_scaled(hid[:, t, :], g1[t], idx6[:], sb_t, t)
+        for half in range(2):
+            fetch_scaled(hid[:, LAST, half * P : (half + 1) * P], g1[LAST], list_half(idx6, O, half), sb_t, LAST)
+        woven = [keep.tile([P, P, PACK], BF16, name=f"woven{half}", align_bytes=ALIGN) for half in range(2)]
+        hid_w = [keep.tile([P, P], U32, name=f"hid_w{half}", align_bytes=ALIGN) for half in range(2)]
+        hid_s = [keep.tile([P, P], U8, name=f"hid_s{half}", align_bytes=ALIGN) for half in range(2)]
         out_v = out.rearrange("(b p) o -> p b o", p=P)
-        for h in range(2):
+        for half in range(2):
+            places = slice(half * P, (half + 1) * P)
             nc.vector.tensor_copy(
-                woven[h][:].rearrange("p (c i) t -> p c t i", i=4),
-                hid[:, :, h * P : (h + 1) * P].rearrange("p t (c i) -> p c t i", i=4))
-            nc.vector.quantize_mx(out=hid_w[h][:].bitcast(FP8X4), scales=hid_s[h][:], in_=woven[h][:].rearrange("p o t -> p (o t)"))
+                woven[half][:].rearrange("p (c i) t -> p c t i", i=4),
+                hid[:, :, places].rearrange("p t (c i) -> p c t i", i=4))
+            nc.vector.quantize_mx(
+                out=hid_w[half][:].bitcast(FP8X4), scales=hid_s[half][:],
+                in_=woven[half][:].rearrange("p o t -> p (o t)"))
             for b in range(2):
                 nc.tensor.matmul_mx(
-                    out=banks[h][:, b, :], lhsT=wb_w[:, 2 * b * P : 2 * (b + 1) * P].bitcast(FP4X4), lhsT_scale=wb_sc[:, b * P : (b + 1) * P],
-                    rhs=hid_w[h][:].bitcast(FP8X4), rhs_scale=hid_s[h][:],
+                    out=y_ps[half][:, b, :],
+                    lhsT=wb_w[:, 2 * b * P : 2 * (b + 1) * P].bitcast(FP4X4), lhsT_scale=wb_s[:, b * P : (b + 1) * P],
+                    rhs=hid_w[half][:].bitcast(FP8X4), rhs_scale=hid_s[half][:],
                     start=False, stop=(b == 1))
-            y_sb = keep.tile([P, 2, P], F32, name=f"y_sb{h}")
-            if h == 0:
-                nc.scalar.copy(y_sb[:], banks[h][:])
+            y_sb = keep.tile([P, 2, P], F32, name=f"y_sb{half}")
+            if half == 0:
+                nc.scalar.copy(y_sb[:], y_ps[half][:])
             else:
-                nc.vector.tensor_copy(y_sb[:], banks[h][:])
-            nc.sync.dma_start(out_v[:, :, h * P : (h + 1) * P], y_sb[:])
+                nc.vector.tensor_copy(y_sb[:], y_ps[half][:])
+            nc.sync.dma_start(out_v[:, :, places], y_sb[:])

from contextlib import ExitStack

import concourse.mybir as mybir

K, J, R, T, F, O, C, S, N = 512, 512, 512, 1024, 1024, 256, 512, 256, 256
FLOPS = 2 * K * R * J + 2 * R * N * O + 2 * K * N * O

F32 = mybir.dt.float32
BF16 = mybir.dt.bfloat16
I32 = mybir.dt.int32
U32 = mybir.dt.uint32
U16 = mybir.dt.uint16
U8 = mybir.dt.uint8
FP8X4 = mybir.dt.float8_e4m3fn_x4
FP4X4 = mybir.dt.float4_e2m1fn_x4
COPY = mybir.ActivationFunctionType.Copy
RELU = mybir.ActivationFunctionType.Relu
ADD = mybir.AluOpType.add

P = 128
PACK = 4
QUADS = 4
QUAD = 32
SCALE_ROWS = 4
LIST_COL = 16
ALIGN = 64
LAST = PACK - 1


def tile_picked_tokens_twobooks_one_weighedposting_further_plain_kernel(
    tc, xt_words, xt_scales, ua, ub, ha, hb, sa, sb, wb_words, wb_scales, ws_words, ws_scales,
    offs, offs2, offs3, offs4, offs5, offs6, offs7, out,
):
    nc = tc.nc
    with ExitStack() as ctx:
        keep = ctx.enter_context(tc.tile_pool(name="keep", bufs=1))
        psum = ctx.enter_context(tc.psum_pool(name="psum", bufs=1))

        def load_list(src, name):
            tile = keep.tile(list(src.shape), U16, name=name)
            nc.sync.dma_start(tile[:], src)
            return tile

        def load_factors(queue, src, name):
            tile = keep.tile([P, PACK], F32, name=name)
            queue.dma_start(tile[:], src.rearrange("(p j) one -> p (j one)", j=PACK))
            return tile

        def load_plane(src, j, name):
            tile = keep.tile([P, F], F32, name=name)
            nc.sync.dma_start(tile[:], src.rearrange("(p j) f -> p j f", j=PACK)[:, j, :])
            return tile

        def load_scale_rows(tile, src):
            for q in range(QUADS):
                nc.sync.dma_start(
                    tile[QUAD * q : QUAD * q + SCALE_ROWS, :].bitcast(I32),
                    src[0][SCALE_ROWS * q : SCALE_ROWS * (q + 1), :].bitcast(I32))

        def fetch_scaled(dst, window, offsets, factors, plane):
            nc.scalar.activation(dst, window[:].indirect(offsets), COPY, scale=factors[:, plane : plane + 1])

        def list_half(tile, entries, half):
            cols = entries // 2 // LIST_COL
            return tile[:, half * cols : (half + 1) * cols]

        warm_in = keep.tile([P, 1], F32, name="warm_in")
        warm_out = keep.tile([P, 1], F32, name="warm_out")
        nc.vector.memset(warm_in[:], 0.0)
        nc.scalar.activation(warm_out[:], warm_in[:], COPY)

        xt_s = keep.tile([P, T], U8, name="xt_s", align_bytes=ALIGN)
        nc.vector.memset(xt_s[:].bitcast(I32), 0)
        ws_s = keep.tile([P, N], U8, name="ws_s", align_bytes=ALIGN)
        wb_s = keep.tile([P, N], U8, name="wb_s", align_bytes=ALIGN)
        nc.vector.memset(ws_s[:].bitcast(I32), 0)
        nc.vector.memset(wb_s[:].bitcast(I32), 0)
        boards = [keep.tile([P, C], F32, name=f"board{t}") for t in range(PACK)]
        for t in range(PACK):
            nc.vector.memset(boards[t][:], 0.0)

        ha_t = load_factors(nc.scalar, ha, "ha_t")
        hb_t = load_factors(nc.scalar, hb, "hb_t")
        xt_s_stage = keep.tile([SCALE_ROWS, QUADS, T // 4], I32, name="xt_s_stage")
        nc.scalar.dma_start(xt_s_stage[:], xt_scales[0].bitcast(I32).rearrange("(q i) c -> i q c", i=SCALE_ROWS))
        ua_t, ub_t = [], []
        ua_t.append(load_plane(ua, 0, "ua0"))
        idx2 = load_list(offs2, "idx2")
        ub_t.append(load_plane(ub, 0, "ub0"))
        idx3 = load_list(offs3, "idx3")
        ua_t.append(load_plane(ua, 1, "ua1"))
        idx = load_list(offs, "idx")
        idx7 = load_list(offs7, "idx7")
        xt_w = keep.tile([P, T], U16, name="xt_w", align_bytes=ALIGN)
        nc.sync.dma_start(xt_w[:].bitcast(I32), xt_words[0].bitcast(I32))
        ub_t.append(load_plane(ub, 1, "ub1"))
        for j in range(2, PACK):
            ua_t.append(load_plane(ua, j, f"ua{j}"))
            ub_t.append(load_plane(ub, j, f"ub{j}"))
        sa_t = load_factors(nc.sync, sa, "sa_t")
        idx4 = load_list(offs4, "idx4")
        idx5 = load_list(offs5, "idx5")
        idx6 = load_list(offs6, "idx6")
        sb_t = load_factors(nc.sync, sb, "sb_t")
        ws_w = keep.tile([P, N], U32, name="ws_w", align_bytes=ALIGN)
        nc.sync.dma_start(ws_w[:].bitcast(I32), ws_words[0].rearrange("p n t -> p (n t)").bitcast(I32))
        load_scale_rows(ws_s, ws_scales)
        wb_w = keep.tile([P, 2 * N], U8, name="wb_w", align_bytes=ALIGN)
        nc.sync.dma_start(wb_w[:].bitcast(I32), wb_words[0].bitcast(I32))
        load_scale_rows(wb_s, wb_scales)

        for q in range(QUADS):
            nc.vector.tensor_copy(xt_s[QUAD * q : QUAD * q + SCALE_ROWS, :].bitcast(I32), xt_s_stage[:, q, :])
        slot_w = keep.tile([P, J], U16, name="slot_w", align_bytes=ALIGN)
        slot_s = keep.tile([P, J], U8, name="slot_s", align_bytes=ALIGN)
        place_w = keep.tile([P, O], U16, name="place_w", align_bytes=ALIGN)
        place_s = keep.tile([P, O], U8, name="place_s", align_bytes=ALIGN)
        nc.vector.tensor_copy(slot_s[:], xt_s[:].indirect(idx[:]))
        nc.vector.tensor_copy(place_s[:], xt_s[:].indirect(idx7[:]))
        nc.vector.tensor_copy(slot_w[:], xt_w[:].indirect(idx[:]))
        nc.vector.tensor_copy(place_w[:], xt_w[:].indirect(idx7[:]))

        from_a = [keep.tile([P, 2, R], F32, name=f"from_a{u}") for u in range(2)]
        from_b = [keep.tile([P, 2, R], F32, name=f"from_b{u}") for u in range(2)]
        wc = keep.tile([P, R, PACK], BF16, name="wc", align_bytes=ALIGN)
        wc_v = wc[:].rearrange("p (t m) j -> p m t j", t=PACK)
        a_v = [tile[:].rearrange("p e (m t) -> p m t e", t=PACK) for tile in from_a]
        b_v = [tile[:].rearrange("p e (m t) -> p m t e", t=PACK) for tile in from_b]
        half_r = R // 2
        for j in range(PACK):
            u, e = divmod(j, 2)
            fetch_scaled(from_a[u][:, e, :], ua_t[j], idx2[:], ha_t, j)
            if j < LAST:
                fetch_scaled(from_b[u][:, e, :], ub_t[j], idx3[:], hb_t, j)
            else:
                for half in range(2):
                    fetch_scaled(from_b[u][:, e, half * half_r : (half + 1) * half_r], ub_t[j],
                                 list_half(idx3, R, half), hb_t, j)
            if j == 1:
                nc.vector.tensor_tensor(wc_v[:, :, :, 0:2], a_v[0], b_v[0], ADD)

        wc_w = [keep.tile([P, P], U32, name=f"wc_w{t}", align_bytes=ALIGN) for t in range(PACK)]
        wc_s = [keep.tile([P, P], U8, name=f"wc_s{t}", align_bytes=ALIGN) for t in range(PACK)]
        half_m = P // 2
        for t in range(PACK):
            if t % 2 == 0:
                for half in range(2):
                    ms, ts = slice(half * half_m, (half + 1) * half_m), slice(t, t + 2)
                    nc.vector.tensor_tensor(
                        wc_v[:, ms, ts, 2:4].rearrange("p m t e -> p m e t"),
                        a_v[1][:, ms, ts, :].rearrange("p m t e -> p m e t"),
                        b_v[1][:, ms, ts, :].rearrange("p m t e -> p m e t"), ADD)
            nc.vector.quantize_mx(
                out=wc_w[t][:].bitcast(FP8X4), scales=wc_s[t][:],
                in_=wc[:, t * P : (t + 1) * P, :].rearrange("p m j -> p (m j)"))

        for t in range(PACK):
            a_sb = keep.tile([P, J], F32, name=f"a_sb{t}", tag="rows", bufs=2, align_bytes=ALIGN)
            pieces = 2 if t == 0 else 1
            width = J // pieces
            for i in range(pieces):
                cols = slice(i * width, (i + 1) * width)
                a_ps = psum.tile([P, width], F32, name=f"a_ps{t}_{i}")
                nc.tensor.matmul_mx(
                    out=a_ps[:], lhsT=wc_w[t][:].bitcast(FP8X4), lhsT_scale=wc_s[t][:],
                    rhs=slot_w[:, cols].bitcast(FP4X4), rhs_scale=slot_s[:, cols],
                    start=True, stop=True)
                if t == 1:
                    nc.vector.tensor_copy(a_sb[:, cols], a_ps[:])
                else:
                    nc.scalar.copy(a_sb[:, cols], a_ps[:])
            h1 = keep.tile([P, S], F32, name=f"h1_{t}")
            fetch_scaled(h1[:], a_sb, idx4[:], sa_t, t)
            if t == 0:
                nc.vector.tensor_copy(boards[t][:].indirect(idx5[:]), h1[:])
            else:
                h1_pos = keep.tile([P, S], F32, name=f"h1_pos{t}")
                nc.scalar.activation(h1_pos[:], h1[:], RELU)
                nc.vector.tensor_copy(boards[t][:].indirect(idx5[:]), h1_pos[:])
        g1_0 = keep.tile([P, C], F32, name="g1_0", tag="rows", bufs=2, align_bytes=ALIGN)
        nc.scalar.activation(g1_0[:], boards[0][:], RELU)
        g1 = [g1_0] + boards[1:]

        y_ps = [psum.tile([P, 2, P], F32, name=f"y_ps{half}") for half in range(2)]
        for half in range(2):
            places = slice(half * P, (half + 1) * P)
            for b in range(2):
                nc.tensor.matmul_mx(
                    out=y_ps[half][:, b, :],
                    lhsT=ws_w[:, b * P : (b + 1) * P].bitcast(FP8X4), lhsT_scale=ws_s[:, b * P : (b + 1) * P],
                    rhs=place_w[:, places].bitcast(FP4X4), rhs_scale=place_s[:, places],
                    start=(b == 0), stop=False)

        hid = keep.tile([P, PACK, O], BF16, name="hid", tag="rows", bufs=2, align_bytes=ALIGN)
        for t in range(LAST):
            fetch_scaled(hid[:, t, :], g1[t], idx6[:], sb_t, t)
        for half in range(2):
            fetch_scaled(hid[:, LAST, half * P : (half + 1) * P], g1[LAST], list_half(idx6, O, half), sb_t, LAST)
        woven = [keep.tile([P, P, PACK], BF16, name=f"woven{half}", align_bytes=ALIGN) for half in range(2)]
        hid_w = [keep.tile([P, P], U32, name=f"hid_w{half}", align_bytes=ALIGN) for half in range(2)]
        hid_s = [keep.tile([P, P], U8, name=f"hid_s{half}", align_bytes=ALIGN) for half in range(2)]
        out_v = out.rearrange("(b p) o -> p b o", p=P)
        for half in range(2):
            places = slice(half * P, (half + 1) * P)
            nc.vector.tensor_copy(
                woven[half][:].rearrange("p (c i) t -> p c t i", i=4),
                hid[:, :, places].rearrange("p t (c i) -> p c t i", i=4))
            nc.vector.quantize_mx(
                out=hid_w[half][:].bitcast(FP8X4), scales=hid_s[half][:],
                in_=woven[half][:].rearrange("p o t -> p (o t)"))
            for b in range(2):
                nc.tensor.matmul_mx(
                    out=y_ps[half][:, b, :],
                    lhsT=wb_w[:, 2 * b * P : 2 * (b + 1) * P].bitcast(FP4X4), lhsT_scale=wb_s[:, b * P : (b + 1) * P],
                    rhs=hid_w[half][:].bitcast(FP8X4), rhs_scale=hid_s[half][:],
                    start=False, stop=(b == 1))
            y_sb = keep.tile([P, 2, P], F32, name=f"y_sb{half}")
            if half == 0:
                nc.scalar.copy(y_sb[:], y_ps[half][:])
            else:
                nc.vector.tensor_copy(y_sb[:], y_ps[half][:])
            nc.sync.dma_start(out_v[:, :, places], y_sb[:])
